import numpy as np, ml_dtypes
CORES = [4,12,20,28,36,44,52,60,132,140,148,156,164,172,180,188]
N = 16
def setup_inputs(rng):
    return {"x1": rng.standard_normal((N, 128, 32), dtype=np.float32), "x2": rng.standard_normal((N, 128, 2048), dtype=np.float32).astype(ml_dtypes.bfloat16)}
def reference(x1, x2):
    out = []
    s = x1.sum(axis=0, dtype=np.float64).astype(x1.dtype)
    out.append(np.broadcast_to(s, (N,) + s.shape))
    out.append(np.broadcast_to(x2[8], x2.shape))
    return {"y1": out[0], "y2": out[1]}

@@ -1,0 +1,121 @@
+from concourse.bass import DstId, RemoteDMATransfer
+from concourse.mybir import AluOpType
+
+SCRATCH = {
+    "b2": ("dram", [32, 128, 64], "bfloat16"),
+    "x1s": ("dram", [8, 128, 4], "float32"),
+    "r1": ("dram", [8, 128, 4], "float32"),
+    "s1e": ("dram", [8, 128, 4], "float32"),
+    "s1o": ("dram", [8, 128, 4], "float32"),
+}
+SEMAPHORES = ["gl", "snt", "r1in", "sume", "sumo", "ld0", "ld1", "ld2", "ld3", "hand", "piece",
+              "got0", "got1", "got2", "got3", "sta", "stb"]
+
+ROOT = 132
+SCATTERER = {0: 132, 1: 131, 2: 134, 3: 130}
+HOLDER_CORE = (6, 2)
+
+
+def plane(par):
+    return [h * 128 + ch * 8 for h in (0, 1) for ch in range(par, 8, 2)]
+
+
+def rank_program(g, core, T, topo):
+    sem = T.sem
+    local = core % 8
+    ch = topo.chip(core)
+    if ch >= 8:
+        return
+    par = ch % 2
+    k_own = plane(par).index(core - local)
+    ranks = list(T.cores)
+
+    def did(d):
+        rid, pid = topo.addr(d, core)
+        return DstId(rid=rid, pnc=pid)
+
+    def scatter(q):
+        hc = HOLDER_CORE[q % 2]
+        g.remote_dma_fused(
+            [RemoteDMATransfer(dst_ids=[did(base + hc)], dma_engine_mask=1 << k, remote_sem=sem.piece,
+                               src=T.b2[8 * q + k], dst=T.b2[8 * q + k])
+             for k, base in enumerate(plane(q // 2))], local_sem=sem.snt)
+        return 8
+
+    def hold(q):
+        p = 8 * q + k_own
+        dsts = [r for r in ranks if r != ROOT]
+        g.wait_ge(sem.piece, 1)
+        g.remote_dma_fused(
+            [RemoteDMATransfer(dst_ids=[did(r) for r in dsts], dma_engine_mask=0xFF, remote_sem=sem["got%d" % q],
+                               srcs=[T.b2[p]], dsts=[T.b2[p] for r in dsts])], local_sem=sem.snt)
+        return 8
+
+    if local == 7:
+        g.wait_ge(sem.r1in, 8)
+        out = T.s1o if par else T.s1e
+        g.remote_dma_fused(
+            [RemoteDMATransfer(dst_ids=[did(r) for r in ranks], dma_engine_mask=0xFF,
+                               remote_sem=sem.sumo if par else sem.sume,
+                               srcs=[T.r1[j] for j in range(8)], dsts=[out[k_own] for r in ranks], alu_op=1)],
+            local_sem=sem.snt)
+        g.wait_ge(sem.snt, 8)
+        return
+
+    if local in (6, 2) or core == 131:
+        sent = 0
+        for q, s in SCATTERER.items():
+            if s == core:
+                g.wait_ge(sem.hand, 16)
+                sent += scatter(q)
+        if local in (6, 2):
+            sent += hold(2 * par + HOLDER_CORE.index(local))
+        g.wait_ge(sem.snt, sent)
+        return
+
+    if local != 4:
+        return
+
+    sent = 0
+    if core == ROOT:
+        g.sync.dma_start(T.b2[16:24], T.x2[64:96, :]).then_inc(sem.ld2, 16)
+        g.scalar.dma_start(T.b2[24:32], T.x2[96:128, :]).then_inc(sem.ld3, 16)
+        g.sync.dma_start(T.b2[8:16], T.x2[32:64, :]).then_inc(sem.ld1, 16)
+        g.scalar.dma_start(T.b2[0:8], T.x2[0:32, :]).then_inc(sem.ld0, 16)
+        g.sync.dma_start(T.y2[0:64, :], T.x2[0:64, :]).then_inc(sem.sta, 16)
+        g.scalar.dma_start(T.y2[64:128, :], T.x2[64:128, :]).then_inc(sem.stb, 16)
+        g.sync.wait_ge(sem.sta, 16)
+        g.scalar.wait_ge(sem.stb, 16)
+    else:
+        for q, eng, st in ((0, g.sync, sem.sta), (2, g.scalar, sem.stb), (1, g.sync, sem.sta), (3, g.scalar, sem.stb)):
+            eng.wait_ge(sem["got%d" % q], 64)
+            eng.dma_start(T.y2[32 * q:32 * q + 32, :], T.b2[8 * q:8 * q + 8]).then_inc(st, 16)
+        g.sync.wait_ge(sem.sta, 32)
+        g.scalar.wait_ge(sem.stb, 32)
+
+    g.dma_start(T.x1s[:], T.x1[:]).then_inc(sem.gl, 16)
+    g.wait_ge(sem.gl, 16)
+    g.remote_dma_fused(
+        [RemoteDMATransfer(dst_ids=[did(base + 7)], dma_engine_mask=1 << k, remote_sem=sem.r1in,
+                           src=T.x1s[k], dst=T.r1[k_own])
+         for k, base in enumerate(plane(par))], local_sem=sem.snt)
+    sent += 8
+
+    if core == ROOT:
+        for q in (2, 3, 1):
+            g.wait_ge(sem["ld%d" % q], 16)
+            g.remote_dma_fused(
+                [RemoteDMATransfer(dst_ids=[did(SCATTERER[q])], dma_engine_mask=3 << (2 * k), remote_sem=sem.hand,
+                                   src=T.b2[8 * q + k], dst=T.b2[8 * q + k]) for k in range(8)], local_sem=sem.snt)
+            sent += 16
+        g.wait_ge(sem.ld0, 16)
+        sent += scatter(0)
+
+    own, oth = (T.s1o, T.s1e) if par else (T.s1e, T.s1o)
+    g.wait_ge(sem.sumo if par else sem.sume, 64)
+    g.dma_start(T.y1[:], own[:]).then_inc(sem.gl, 16)
+    g.wait_ge(sem.gl, 32)
+    g.wait_ge(sem.sume if par else sem.sumo, 64)
+    g.dma_start(T.y1[:], oth[:], accum_op=AluOpType.add).then_inc(sem.gl, 16)
+    g.wait_ge(sem.gl, 48)
+    g.wait_ge(sem.snt, sent)

@@ -1,23 +1,30 @@
 from concourse.bass import DstId, RemoteDMATransfer
-from concourse.mybir import AluOpType
 
+NE, NO = 32, 36
 SCRATCH = {
-    "b2": ("dram", [32, 128, 64], "bfloat16"),
+    "be": ("dram", [28, 128, NE], "bfloat16"),
+    "bo": ("dram", [32, 128, NO], "bfloat16"),
     "x1s": ("dram", [8, 128, 4], "float32"),
     "r1": ("dram", [8, 128, 4], "float32"),
-    "s1e": ("dram", [8, 128, 4], "float32"),
-    "s1o": ("dram", [8, 128, 4], "float32"),
+    "p1": ("dram", [2, 128, 4], "float32"),
+    "s1": ("dram", [8, 128, 4], "float32"),
 }
-SEMAPHORES = ["gl", "snt", "r1in", "sume", "sumo", "ld0", "ld1", "ld2", "ld3", "hand", "piece",
+SEMAPHORES = ["gl", "snt", "r1in", "p1in", "sum1", "ld0", "ld1", "ld2", "ld3", "goy", "hand", "piece",
               "got0", "got1", "got2", "got3", "sta", "stb"]
 
 ROOT = 132
+ROOT_CHIP = 128
 SCATTERER = {0: 132, 1: 131, 2: 134, 3: 130}
-HOLDER_CORE = (6, 2)
+HOLDERS = ((6, 7), (2, 3))
+ROWS = {0: (0, 28), 1: (28, 56), 2: (56, 92), 3: (92, 128)}
 
 
 def plane(par):
     return [h * 128 + ch * 8 for h in (0, 1) for ch in range(par, 8, 2)]
+
+
+def holder_chips(par):
+    return [b for b in plane(par) if b != ROOT_CHIP]
 
 
 def rank_program(g, core, T, topo):
@@ -26,96 +33,112 @@ def rank_program(g, core, T, topo):
     ch = topo.chip(core)
     if ch >= 8:
         return
+    base = core - local
     par = ch % 2
-    k_own = plane(par).index(core - local)
+    k_own = plane(par).index(base)
     ranks = list(T.cores)
+    sent = [0]
 
     def did(d):
         rid, pid = topo.addr(d, core)
         return DstId(rid=rid, pnc=pid)
 
-    def scatter(q):
-        hc = HOLDER_CORE[q % 2]
-        g.remote_dma_fused(
-            [RemoteDMATransfer(dst_ids=[did(base + hc)], dma_engine_mask=1 << k, remote_sem=sem.piece,
-                               src=T.b2[8 * q + k], dst=T.b2[8 * q + k])
-             for k, base in enumerate(plane(q // 2))], local_sem=sem.snt)
-        return 8
+    def fused(transfers, engines):
+        g.remote_dma_fused(transfers, local_sem=sem.snt)
+        sent[0] += engines
 
-    def hold(q):
-        p = 8 * q + k_own
-        dsts = [r for r in ranks if r != ROOT]
-        g.wait_ge(sem.piece, 1)
-        g.remote_dma_fused(
-            [RemoteDMATransfer(dst_ids=[did(r) for r in dsts], dma_engine_mask=0xFF, remote_sem=sem["got%d" % q],
-                               srcs=[T.b2[p]], dsts=[T.b2[p] for r in dsts])], local_sem=sem.snt)
-        return 8
+    def slots(q):
+        n = len(holder_chips(q // 2)) * 2
+        return (T.bo if q // 2 else T.be), (q % 2) * n, n
+
+    def scatter(q):
+        buf, first, n = slots(q)
+        chips = holder_chips(q // 2)
+        for sub in (0, 1):
+            s0 = first + sub * len(chips)
+            fused([RemoteDMATransfer(dst_ids=[did(b + HOLDERS[q % 2][sub])], dma_engine_mask=1 << k,
+                                     remote_sem=sem.piece, src=buf[s0 + k], dst=buf[s0 + k])
+                   for k, b in enumerate(chips)], len(chips))
 
     if local == 7:
         g.wait_ge(sem.r1in, 8)
-        out = T.s1o if par else T.s1e
-        g.remote_dma_fused(
-            [RemoteDMATransfer(dst_ids=[did(r) for r in ranks], dma_engine_mask=0xFF,
-                               remote_sem=sem.sumo if par else sem.sume,
-                               srcs=[T.r1[j] for j in range(8)], dsts=[out[k_own] for r in ranks], alu_op=1)],
-            local_sem=sem.snt)
-        g.wait_ge(sem.snt, 8)
-        return
+        fused([RemoteDMATransfer(dst_ids=[did(base + 1), did((base ^ 8) + 1)], dma_engine_mask=1, remote_sem=sem.p1in,
+                                 srcs=[T.r1[j] for j in range(8)], dsts=[T.p1[par], T.p1[par]], alu_op=1)], 1)
 
-    if local in (6, 2) or core == 131:
-        sent = 0
+    if local == 1:
+        g.wait_ge(sem.p1in, 2)
+        fused([RemoteDMATransfer(dst_ids=[did(b + 4)], dma_engine_mask=1 << k, remote_sem=sem.sum1,
+                                 srcs=[T.p1[0], T.p1[1]], dsts=[T.s1[k_own]], alu_op=1)
+               for k, b in enumerate(plane(par))], 8)
+
+    if base == ROOT_CHIP and local != 4:
         for q, s in SCATTERER.items():
             if s == core:
-                g.wait_ge(sem.hand, 16)
-                sent += scatter(q)
-        if local in (6, 2):
-            sent += hold(2 * par + HOLDER_CORE.index(local))
-        g.wait_ge(sem.snt, sent)
-        return
+                g.wait_ge(sem.hand, slots(q)[2])
+                scatter(q)
+    elif local in (2, 3, 6, 7):
+        die = 0 if local in HOLDERS[0] else 1
+        sub = HOLDERS[die].index(local)
+        q = 2 * par + die
+        buf, first, n = slots(q)
+        chips = holder_chips(par)
+        s = first + sub * len(chips) + chips.index(base)
+        dsts = [r for r in ranks if r != ROOT]
+        rot = (2 * s) % len(dsts)
+        dsts = dsts[rot:] + dsts[:rot]
+        g.wait_ge(sem.piece, 1)
+        fused([RemoteDMATransfer(dst_ids=[did(r) for r in dsts[2 * e:2 * e + 2]], dma_engine_mask=1 << e,
+                                 remote_sem=sem["got%d" % q], srcs=[buf[s]], dsts=[buf[s] for r in dsts[2 * e:2 * e + 2]])
+               for e in range(8)], 8)
 
     if local != 4:
+        if sent[0]:
+            g.wait_ge(sem.snt, sent[0])
         return
 
-    sent = 0
+    def quarter(q):
+        buf, first, n = slots(q)
+        return buf[first:first + n]
+
+    def rows(t, q):
+        return t[ROWS[q][0]:ROWS[q][1], :]
+
     if core == ROOT:
-        g.sync.dma_start(T.b2[16:24], T.x2[64:96, :]).then_inc(sem.ld2, 16)
-        g.scalar.dma_start(T.b2[24:32], T.x2[96:128, :]).then_inc(sem.ld3, 16)
-        g.sync.dma_start(T.b2[8:16], T.x2[32:64, :]).then_inc(sem.ld1, 16)
-        g.scalar.dma_start(T.b2[0:8], T.x2[0:32, :]).then_inc(sem.ld0, 16)
+        g.sync.dma_start(quarter(2), rows(T.x2, 2)).then_inc(sem.ld2, 16)
+        g.scalar.dma_start(quarter(3), rows(T.x2, 3)).then_inc(sem.ld3, 16)
+        g.sync.dma_start(quarter(1), rows(T.x2, 1)).then_inc(sem.ld1, 16)
+        g.scalar.dma_start(quarter(0), rows(T.x2, 0)).then_inc(sem.ld0, 16)
+        g.sync.wait_ge(sem.sum1, 8)
+        g.sync.dma_start(T.y1[:], T.s1[:]).then_inc(sem.sta, 16)
+        g.sync.wait_ge(sem.goy, 1)
         g.sync.dma_start(T.y2[0:64, :], T.x2[0:64, :]).then_inc(sem.sta, 16)
+        g.scalar.wait_ge(sem.goy, 1)
         g.scalar.dma_start(T.y2[64:128, :], T.x2[64:128, :]).then_inc(sem.stb, 16)
-        g.sync.wait_ge(sem.sta, 16)
+        g.sync.wait_ge(sem.sta, 32)
         g.scalar.wait_ge(sem.stb, 16)
     else:
-        for q, eng, st in ((0, g.sync, sem.sta), (2, g.scalar, sem.stb), (1, g.sync, sem.sta), (3, g.scalar, sem.stb)):
-            eng.wait_ge(sem["got%d" % q], 64)
-            eng.dma_start(T.y2[32 * q:32 * q + 32, :], T.b2[8 * q:8 * q + 8]).then_inc(st, 16)
+        for q, eng, st in ((2, g.sync, sem.sta), (3, g.scalar, sem.stb), (1, g.sync, sem.sta), (0, g.scalar, sem.stb)):
+            eng.wait_ge(sem["got%d" % q], slots(q)[2])
+            eng.dma_start(rows(T.y2, q), quarter(q)).then_inc(st, 16)
         g.sync.wait_ge(sem.sta, 32)
         g.scalar.wait_ge(sem.stb, 32)
 
     g.dma_start(T.x1s[:], T.x1[:]).then_inc(sem.gl, 16)
     g.wait_ge(sem.gl, 16)
-    g.remote_dma_fused(
-        [RemoteDMATransfer(dst_ids=[did(base + 7)], dma_engine_mask=1 << k, remote_sem=sem.r1in,
-                           src=T.x1s[k], dst=T.r1[k_own])
-         for k, base in enumerate(plane(par))], local_sem=sem.snt)
-    sent += 8
+    fused([RemoteDMATransfer(dst_ids=[did(b + 7)], dma_engine_mask=1 << k, remote_sem=sem.r1in,
+                             src=T.x1s[k], dst=T.r1[k_own]) for k, b in enumerate(plane(par))], 8)
 
     if core == ROOT:
         for q in (2, 3, 1):
+            buf, first, n = slots(q)
             g.wait_ge(sem["ld%d" % q], 16)
-            g.remote_dma_fused(
-                [RemoteDMATransfer(dst_ids=[did(SCATTERER[q])], dma_engine_mask=3 << (2 * k), remote_sem=sem.hand,
-                                   src=T.b2[8 * q + k], dst=T.b2[8 * q + k]) for k in range(8)], local_sem=sem.snt)
-            sent += 16
+            fused([RemoteDMATransfer(dst_ids=[did(SCATTERER[q])], dma_engine_mask=1 << k, remote_sem=sem.hand,
+                                     src=buf[first + k], dst=buf[first + k]) for k in range(n)], n)
         g.wait_ge(sem.ld0, 16)
-        sent += scatter(0)
-
-    own, oth = (T.s1o, T.s1e) if par else (T.s1e, T.s1o)
-    g.wait_ge(sem.sumo if par else sem.sume, 64)
-    g.dma_start(T.y1[:], own[:]).then_inc(sem.gl, 16)
-    g.wait_ge(sem.gl, 32)
-    g.wait_ge(sem.sume if par else sem.sumo, 64)
-    g.dma_start(T.y1[:], oth[:], accum_op=AluOpType.add).then_inc(sem.gl, 16)
-    g.wait_ge(sem.gl, 48)
-    g.wait_ge(sem.snt, sent)
+        scatter(0)
+        g.sem_inc(sem.goy, 1)
+    else:
+        g.wait_ge(sem.sum1, 8)
+        g.dma_start(T.y1[:], T.s1[:]).then_inc(sem.gl, 16)
+        g.wait_ge(sem.gl, 32)
+    g.wait_ge(sem.snt, sent[0])

from concourse.bass import DstId, RemoteDMATransfer

NE, NO = 32, 36
SCRATCH = {
    "be": ("dram", [28, 128, NE], "bfloat16"),
    "bo": ("dram", [32, 128, NO], "bfloat16"),
    "x1s": ("dram", [8, 128, 4], "float32"),
    "r1": ("dram", [8, 128, 4], "float32"),
    "p1": ("dram", [2, 128, 4], "float32"),
    "s1": ("dram", [8, 128, 4], "float32"),
}
SEMAPHORES = ["gl", "snt", "r1in", "p1in", "sum1", "ld0", "ld1", "ld2", "ld3", "goy", "hand", "piece",
              "got0", "got1", "got2", "got3", "sta", "stb"]

ROOT = 132
ROOT_CHIP = 128
SCATTERER = {0: 132, 1: 131, 2: 134, 3: 130}
HOLDERS = ((6, 7), (2, 3))
ROWS = {0: (0, 28), 1: (28, 56), 2: (56, 92), 3: (92, 128)}


def plane(par):
    return [h * 128 + ch * 8 for h in (0, 1) for ch in range(par, 8, 2)]


def holder_chips(par):
    return [b for b in plane(par) if b != ROOT_CHIP]


def rank_program(g, core, T, topo):
    sem = T.sem
    local = core % 8
    ch = topo.chip(core)
    if ch >= 8:
        return
    base = core - local
    par = ch % 2
    k_own = plane(par).index(base)
    ranks = list(T.cores)
    sent = [0]

    def did(d):
        rid, pid = topo.addr(d, core)
        return DstId(rid=rid, pnc=pid)

    def fused(transfers, engines):
        g.remote_dma_fused(transfers, local_sem=sem.snt)
        sent[0] += engines

    def slots(q):
        n = len(holder_chips(q // 2)) * 2
        return (T.bo if q // 2 else T.be), (q % 2) * n, n

    def scatter(q):
        buf, first, n = slots(q)
        chips = holder_chips(q // 2)
        for sub in (0, 1):
            s0 = first + sub * len(chips)
            fused([RemoteDMATransfer(dst_ids=[did(b + HOLDERS[q % 2][sub])], dma_engine_mask=1 << k,
                                     remote_sem=sem.piece, src=buf[s0 + k], dst=buf[s0 + k])
                   for k, b in enumerate(chips)], len(chips))

    if local == 7:
        g.wait_ge(sem.r1in, 8)
        fused([RemoteDMATransfer(dst_ids=[did(base + 1), did((base ^ 8) + 1)], dma_engine_mask=1, remote_sem=sem.p1in,
                                 srcs=[T.r1[j] for j in range(8)], dsts=[T.p1[par], T.p1[par]], alu_op=1)], 1)

    if local == 1:
        g.wait_ge(sem.p1in, 2)
        fused([RemoteDMATransfer(dst_ids=[did(b + 4)], dma_engine_mask=1 << k, remote_sem=sem.sum1,
                                 srcs=[T.p1[0], T.p1[1]], dsts=[T.s1[k_own]], alu_op=1)
               for k, b in enumerate(plane(par))], 8)

    if base == ROOT_CHIP and local != 4:
        for q, s in SCATTERER.items():
            if s == core:
                g.wait_ge(sem.hand, slots(q)[2])
                scatter(q)
    elif local in (2, 3, 6, 7):
        die = 0 if local in HOLDERS[0] else 1
        sub = HOLDERS[die].index(local)
        q = 2 * par + die
        buf, first, n = slots(q)
        chips = holder_chips(par)
        s = first + sub * len(chips) + chips.index(base)
        dsts = [r for r in ranks if r != ROOT]
        rot = (2 * s) % len(dsts)
        dsts = dsts[rot:] + dsts[:rot]
        g.wait_ge(sem.piece, 1)
        fused([RemoteDMATransfer(dst_ids=[did(r) for r in dsts[2 * e:2 * e + 2]], dma_engine_mask=1 << e,
                                 remote_sem=sem["got%d" % q], srcs=[buf[s]], dsts=[buf[s] for r in dsts[2 * e:2 * e + 2]])
               for e in range(8)], 8)

    if local != 4:
        if sent[0]:
            g.wait_ge(sem.snt, sent[0])
        return

    def quarter(q):
        buf, first, n = slots(q)
        return buf[first:first + n]

    def rows(t, q):
        return t[ROWS[q][0]:ROWS[q][1], :]

    if core == ROOT:
        g.sync.dma_start(quarter(2), rows(T.x2, 2)).then_inc(sem.ld2, 16)
        g.scalar.dma_start(quarter(3), rows(T.x2, 3)).then_inc(sem.ld3, 16)
        g.sync.dma_start(quarter(1), rows(T.x2, 1)).then_inc(sem.ld1, 16)
        g.scalar.dma_start(quarter(0), rows(T.x2, 0)).then_inc(sem.ld0, 16)
        g.sync.wait_ge(sem.sum1, 8)
        g.sync.dma_start(T.y1[:], T.s1[:]).then_inc(sem.sta, 16)
        g.sync.wait_ge(sem.goy, 1)
        g.sync.dma_start(T.y2[0:64, :], T.x2[0:64, :]).then_inc(sem.sta, 16)
        g.scalar.wait_ge(sem.goy, 1)
        g.scalar.dma_start(T.y2[64:128, :], T.x2[64:128, :]).then_inc(sem.stb, 16)
        g.sync.wait_ge(sem.sta, 32)
        g.scalar.wait_ge(sem.stb, 16)
    else:
        for q, eng, st in ((2, g.sync, sem.sta), (3, g.scalar, sem.stb), (1, g.sync, sem.sta), (0, g.scalar, sem.stb)):
            eng.wait_ge(sem["got%d" % q], slots(q)[2])
            eng.dma_start(rows(T.y2, q), quarter(q)).then_inc(st, 16)
        g.sync.wait_ge(sem.sta, 32)
        g.scalar.wait_ge(sem.stb, 32)

    g.dma_start(T.x1s[:], T.x1[:]).then_inc(sem.gl, 16)
    g.wait_ge(sem.gl, 16)
    fused([RemoteDMATransfer(dst_ids=[did(b + 7)], dma_engine_mask=1 << k, remote_sem=sem.r1in,
                             src=T.x1s[k], dst=T.r1[k_own]) for k, b in enumerate(plane(par))], 8)

    if core == ROOT:
        for q in (2, 3, 1):
            buf, first, n = slots(q)
            g.wait_ge(sem["ld%d" % q], 16)
            fused([RemoteDMATransfer(dst_ids=[did(SCATTERER[q])], dma_engine_mask=1 << k, remote_sem=sem.hand,
                                     src=buf[first + k], dst=buf[first + k]) for k in range(n)], n)
        g.wait_ge(sem.ld0, 16)
        scatter(0)
        g.sem_inc(sem.goy, 1)
    else:
        g.wait_ge(sem.sum1, 8)
        g.dma_start(T.y1[:], T.s1[:]).then_inc(sem.gl, 16)
        g.wait_ge(sem.gl, 32)
    g.wait_ge(sem.snt, sent[0])
